import numpy as np
import ml_dtypes


def mxq(x, axis, fmt="e4m3"):
    dtype, down = {"e4m3": (ml_dtypes.float8_e4m3fn, 7), "e5m2": (ml_dtypes.float8_e5m2, 14)}[fmt]
    v = np.moveaxis(np.asarray(x, np.float32).astype(ml_dtypes.bfloat16).astype(np.float64), axis, -1)
    blocks = v.reshape(v.shape[:-1] + (-1, 32))
    amax = np.abs(blocks).max(-1, keepdims=True)
    byte = np.maximum(np.where(amax > 0, np.frexp(amax)[1] - 1 + 127, 0) - down, 1)
    scale = np.exp2(byte - 127.0)
    codes = (blocks / scale).astype(np.float32).astype(dtype).astype(np.float64)
    return np.moveaxis((codes * scale).reshape(v.shape), -1, axis)


WIDE = False


def mx_kscale(k):
    if not WIDE:
        return np.ones(k)
    levels = np.array([18, -18])
    if k % 512:
        return np.exp2(np.random.permutation(np.resize(levels, k // 32))).repeat(32)
    a = np.empty((k // 512, 16))
    for p in range(k // 512):
        a[p, :8] = np.random.permutation(np.resize(levels, 8))
        for g in range(8):
            far = levels[np.abs(levels - a[p, g]) >= 10]
            a[p, g + 8] = far[np.random.randint(len(far))]
    return np.exp2(a.ravel()).repeat(32)


def f64(x):
    return np.asarray(x).astype(np.float64)


def striped(idx):
    return np.tile(np.asarray(idx).reshape(-1, 16).T, (8, 1)).astype(np.uint16)


def unstriped(offs):
    return offs[:16].T.reshape(-1).astype(np.int64)

def planes(y):
    n, m = y.shape
    v = y.astype(np.float32).astype(ml_dtypes.bfloat16).astype(np.float64).reshape(n // 32, 32, m)
    top = np.abs(v).max(1)
    byte = np.clip(np.where(top > 0, np.frexp(top)[1] - 1 + 127 - 7, 1), 1, 254)
    codes = (v * np.exp2(127.0 - byte)[:, None, :]).reshape(n, m).astype(np.float32).astype(ml_dtypes.float8_e4m3fn).view(np.uint8)
    words = codes.reshape(n // 512, 128, 4, m).transpose(0, 1, 3, 2)
    return np.ascontiguousarray(words), np.ascontiguousarray(byte.astype(np.uint8).reshape(n // 512, 16, m))


def setup_inputs():
    n = np.random.standard_normal
    uni = np.random.uniform
    order = np.random.permutation(2048)
    lc = order[:512]
    rc = order[512:1024]
    f_f = mx_kscale(512)
    return {
        "dh": (np.round(n((512, 512)) * 8) / 8 * f_f[:, None]).astype(np.float32),
        "h": (np.round(np.tanh(2.0 * n((512, 512))) * 256) / 256).astype(np.float32),
        "ul": (n((512, 512)) / np.sqrt(512) / f_f[:, None]).astype(np.float32),
        "ur": (n((512, 512)) / np.sqrt(512) / f_f[:, None]).astype(np.float32),
        "loffs": striped(lc),
        "roffs": striped(rc),
    }


def reference(dh, h, ul, ur, loffs, roffs):
    lc = unstriped(loffs)
    rc = unstriped(roffs)
    dz = f64(dh) * (1.0 - np.square(f64(h)))
    q_dz = mxq(dz, 0, "e5m2")
    a = mxq(f64(ul), 0, "e4m3").T @ q_dz
    b = mxq(f64(ur), 0, "e4m3").T @ q_dz
    pa = np.zeros((512, 2048))
    pa[:, lc] = a
    pb = np.zeros((512, 2048))
    pb[:, rc] = b
    out_0 = pa + pb
    return (out_0,) + planes(out_0)

@@ -1,0 +1,175 @@
+from contextlib import ExitStack
+
+import concourse.mybir as mybir
+
+F32 = mybir.dt.float32
+BF16 = mybir.dt.bfloat16
+I32 = mybir.dt.int32
+U32 = mybir.dt.uint32
+U16 = mybir.dt.uint16
+U8 = mybir.dt.uint8
+E4M3X4 = mybir.dt.float8_e4m3fn_x4
+E5M2X4 = mybir.dt.float8_e5m2_x4
+ACT = mybir.ActivationFunctionType
+MULT = mybir.AluOpType.mult
+
+P = 128
+PACK = 4
+PARENTS = 512
+FEATURES = 512
+NODES = 2048
+HALF = 256
+CHUNK = 512
+LIST_COLS = PARENTS // 16
+
+ORDER = (2, 0, 1, 3)
+
+FLOPS = 2 * 2 * 512 * 512 * 512
+
+
+def tile_attend_gtree_tnh_pl_kernel(tc, dh, h, ul, ur, loffs, roffs, out_0, out_1, out_2):
+    nc = tc.nc
+    with ExitStack() as ctx:
+        sb = ctx.enter_context(tc.tile_pool(name="sb", bufs=1))
+        ps = ctx.enter_context(tc.psum_pool(name="ps", bufs=1))
+
+        left_list = sb.tile([P, LIST_COLS], U16, name="left_list")
+        right_list = sb.tile([P, LIST_COLS], U16, name="right_list")
+
+        def load_half(src, c, name):
+            raw = sb.tile([P, PACK, HALF], F32, name=name, align_bytes=64)
+            nc.sync.dma_start(out=raw[:], in_=src.rearrange("(p j) w -> p j w", j=PACK)[:, :, c * HALF : (c + 1) * HALF])
+            return raw
+
+        h_raw, dh_raw = [], []
+        for c in range(2):
+            h_raw.append(load_half(h, c, "h_raw%d" % c))
+            dh_raw.append(load_half(dh, c, "dh_raw%d" % c))
+        ul_raw = [load_half(ul, c, "ul_raw%d" % c) for c in range(2)]
+        nc.sync.dma_start(left_list[:], loffs)
+        ur_raw = [load_half(ur, c, "ur_raw%d" % c) for c in range(2)]
+        nc.sync.dma_start(right_list[:], roffs)
+
+        windows = [sb.tile([P, NODES], F32, name="window%d" % t, align_bytes=64) for t in range(PACK)]
+        for t in ORDER:
+            nc.vector.memset(windows[t][:].bitcast(I32), 0)
+
+        dz_codes = sb.tile([P, PARENTS], U32, name="dz_codes", align_bytes=64)
+        dz_scales = sb.tile([P, PARENTS], U8, name="dz_scales", align_bytes=64)
+        for c in range(2):
+            squares = sb.tile([P, PACK, HALF], F32, name="squares%d" % c, align_bytes=64)
+            nc.scalar.activation(squares[:], h_raw[c][:], ACT.Square)
+            slope = sb.tile([P, PACK, HALF], F32, name="slope%d" % c, align_bytes=64)
+            nc.scalar.activation(slope[:], squares[:], ACT.Copy, bias=1.0, scale=-1.0)
+            dz = sb.tile([P, HALF * PACK], BF16, name="dz%d" % c, align_bytes=64)
+            nc.vector.tensor_tensor(
+                dz[:].rearrange("p (c i j) -> p c j i", i=4, j=PACK),
+                dh_raw[c][:].rearrange("p j (c i) -> p c j i", i=4),
+                slope[:].rearrange("p j (c i) -> p c j i", i=4),
+                MULT,
+            )
+            cols = slice(c * HALF, (c + 1) * HALF)
+            nc.vector.quantize_mx(out=dz_codes[:, cols].bitcast(E5M2X4), scales=dz_scales[:, cols], in_=dz[:])
+
+        def deal(copy, dealt, raw, c, first, count):
+            m0 = (c * HALF + first) // PACK
+            copy(
+                dealt[:].rearrange("p (t m j) -> p m t j", t=PACK, j=PACK)[:, m0 : m0 + count // PACK],
+                raw[:, :, first : first + count].rearrange("p j (m t) -> p m t j", t=PACK),
+            )
+
+        def quantise_weights(codes, scales, dealt, t0, t1):
+            nc.vector.quantize_mx(
+                out=codes[:, t0 * P : t1 * P].bitcast(E4M3X4),
+                scales=scales[:, t0 * P : t1 * P],
+                in_=dealt[:, t0 * P * PACK : t1 * P * PACK],
+            )
+
+        ul_dealt = sb.tile([P, FEATURES * PACK], BF16, name="ul_dealt", align_bytes=64)
+        ul_codes = sb.tile([P, FEATURES], U32, name="ul_codes", tag="ul_codes_then_planes", align_bytes=64)
+        ul_scales = sb.tile([P, FEATURES], U8, name="ul_scales", align_bytes=64)
+        deal(nc.scalar.copy, ul_dealt, ul_raw[0], 0, 0, HALF)
+        deal(nc.vector.tensor_copy, ul_dealt, ul_raw[1], 1, 0, HALF)
+        quantise_weights(ul_codes, ul_scales, ul_dealt, 2, 3)
+        quantise_weights(ul_codes, ul_scales, ul_dealt, 0, 2)
+        quantise_weights(ul_codes, ul_scales, ul_dealt, 3, 4)
+
+        def product(codes, scales, t, bank):
+            acc = ps.tile([P, PARENTS], F32, name="acc", tag="bank%d" % bank)
+            cols = slice(t * P, (t + 1) * P)
+            nc.tensor.matmul_mx(
+                out=acc[:],
+                lhsT=codes[:, cols].bitcast(E4M3X4),
+                lhsT_scale=scales[:, cols],
+                rhs=dz_codes[:].bitcast(E5M2X4),
+                rhs_scale=dz_scales[:],
+                start=True,
+                stop=True,
+            )
+            return acc
+
+        def scatter(acc, offsets, t, first, count, tag):
+            values = sb.tile([P, count], F32, name="values", tag=tag, align_bytes=64)
+            nc.scalar.copy(values[:], acc[:, first : first + count])
+            nc.vector.tensor_copy(windows[t][:].indirect(offsets[:, first // 16 : (first + count) // 16]), values[:])
+
+        first_acc = product(ul_codes, ul_scales, ORDER[0], 0)
+        scatter(first_acc, left_list, ORDER[0], 0, HALF, "values_first")
+
+        ur_dealt = sb.tile([P, FEATURES * PACK], BF16, name="ur_dealt", align_bytes=64)
+        ur_codes = sb.tile([P, FEATURES], U32, name="ur_codes", align_bytes=64)
+        ur_scales = sb.tile([P, FEATURES], U8, name="ur_scales", align_bytes=64)
+        for c in range(2):
+            for first in (0, HALF // 2):
+                deal(nc.scalar.copy, ur_dealt, ur_raw[c], c, first, HALF // 2)
+        quantise_weights(ur_codes, ur_scales, ur_dealt, 0, 4)
+        scatter(first_acc, left_list, ORDER[0], HALF, HALF, "ur_raw1")
+
+        out_rows = out_0.rearrange("(p t) n -> p t n", t=PACK)
+        chunks = [slice(k * CHUNK, (k + 1) * CHUNK) for k in range(NODES // CHUNK)]
+
+        def left(step):
+            t = ORDER[step]
+            scatter(product(ul_codes, ul_scales, t, step), left_list, t, 0, PARENTS, "values_left%d" % step)
+
+        def right(step, tag):
+            t = ORDER[step]
+            scatter(product(ur_codes, ur_scales, t, step + 1), right_list, t, 0, PARENTS, tag)
+            nc.sync.dma_start(out=out_rows[:, t, :], in_=windows[t][:])
+
+        def lane(step):
+            t = ORDER[step]
+            for cols in chunks:
+                nc.scalar.copy(lanes[:, cols, t], windows[t][:, cols])
+
+        right(0, "values_right0")
+        for step in (1, 2):
+            left(step)
+            right(step, "values_right%d" % step)
+        left(3)
+        grouped = sb.tile([P, NODES * PACK], BF16, name="grouped", tag="ul_codes_then_planes", align_bytes=64)
+        lanes = grouped[:].rearrange("p (n t) -> p n t", t=PACK)
+        lane(0)
+        right(3, "values_right0")
+        lane(1)
+        lane(2)
+        last = PACK - 1
+        for k, cols in enumerate(chunks):
+            copy = nc.vector.tensor_copy if k < 2 else nc.scalar.copy
+            copy(lanes[:, cols, last], windows[last][:, cols])
+
+        out_words = out_1[0].rearrange("p n t -> p (n t)").bitcast(I32)
+        out_scales = sb.tile([P, NODES], U8, name="out_scales", align_bytes=64)
+        for k, cols in enumerate(chunks):
+            words = sb.tile([P, CHUNK], U32, name="words%d" % k, align_bytes=64)
+            nc.vector.quantize_mx(
+                out=words[:].bitcast(E4M3X4),
+                scales=out_scales[:, cols],
+                in_=grouped[:, k * CHUNK * PACK : (k + 1) * CHUNK * PACK],
+            )
+            nc.sync.dma_start(out=out_words[:, cols], in_=words[:].bitcast(I32))
+        for q in range(4):
+            nc.scalar.dma_start(
+                out=out_2[0, 4 * q : 4 * q + 4, :].bitcast(I32),
+                in_=out_scales[32 * q : 32 * q + 4, :].bitcast(I32),
+            )

@@ -12,6 +12,7 @@ E4M3X4 = mybir.dt.float8_e4m3fn_x4
 E5M2X4 = mybir.dt.float8_e5m2_x4
 ACT = mybir.ActivationFunctionType
 MULT = mybir.AluOpType.mult
+ADD = mybir.AluOpType.add
 
 P = 128
 PACK = 4
@@ -22,7 +23,7 @@ HALF = 256
 CHUNK = 512
 LIST_COLS = PARENTS // 16
 
-ORDER = (2, 0, 1, 3)
+ORDER = (1, 2, 3, 0)
 
 FLOPS = 2 * 2 * 512 * 512 * 512
 
@@ -41,10 +42,8 @@ def tile_attend_gtree_tnh_pl_kernel(tc, dh, h, ul, ur, loffs, roffs, out_0, out_
             nc.sync.dma_start(out=raw[:], in_=src.rearrange("(p j) w -> p j w", j=PACK)[:, :, c * HALF : (c + 1) * HALF])
             return raw
 
-        h_raw, dh_raw = [], []
-        for c in range(2):
-            h_raw.append(load_half(h, c, "h_raw%d" % c))
-            dh_raw.append(load_half(dh, c, "dh_raw%d" % c))
+        h_raw = [load_half(h, c, "h_raw%d" % c) for c in range(2)]
+        dh_raw = [load_half(dh, c, "dh_raw%d" % c) for c in range(2)]
         ul_raw = [load_half(ul, c, "ul_raw%d" % c) for c in range(2)]
         nc.sync.dma_start(left_list[:], loffs)
         ur_raw = [load_half(ur, c, "ur_raw%d" % c) for c in range(2)]
@@ -60,7 +59,10 @@ def tile_attend_gtree_tnh_pl_kernel(tc, dh, h, ul, ur, loffs, roffs, out_0, out_
             squares = sb.tile([P, PACK, HALF], F32, name="squares%d" % c, align_bytes=64)
             nc.scalar.activation(squares[:], h_raw[c][:], ACT.Square)
             slope = sb.tile([P, PACK, HALF], F32, name="slope%d" % c, align_bytes=64)
-            nc.scalar.activation(slope[:], squares[:], ACT.Copy, bias=1.0, scale=-1.0)
+            if c == 0:
+                nc.vector.tensor_scalar(slope[:], squares[:], -1.0, 1.0, MULT, ADD)
+            else:
+                nc.scalar.activation(slope[:], squares[:], ACT.Copy, bias=1.0, scale=-1.0)
             dz = sb.tile([P, HALF * PACK], BF16, name="dz%d" % c, align_bytes=64)
             nc.vector.tensor_tensor(
                 dz[:].rearrange("p (c i j) -> p c j i", i=4, j=PACK),
@@ -78,29 +80,32 @@ def tile_attend_gtree_tnh_pl_kernel(tc, dh, h, ul, ur, loffs, roffs, out_0, out_
                 raw[:, :, first : first + count].rearrange("p j (m t) -> p m t j", t=PACK),
             )
 
-        def quantise_weights(codes, scales, dealt, t0, t1):
-            nc.vector.quantize_mx(
-                out=codes[:, t0 * P : t1 * P].bitcast(E4M3X4),
-                scales=scales[:, t0 * P : t1 * P],
-                in_=dealt[:, t0 * P * PACK : t1 * P * PACK],
-            )
+        def quantise_weights(dealt, name, first_tag):
+            operands = {}
+            for t0, t1 in ((1, 2), (2, 4), (0, 1)):
+                tag = first_tag if t0 == ORDER[0] else "%s_codes%d" % (name, t0)
+                codes = sb.tile([P, (t1 - t0) * P], U32, name="codes", tag=tag, align_bytes=64)
+                scales = sb.tile([P, (t1 - t0) * P], U8, name="scales", tag="%s_scales%d" % (name, t0), align_bytes=64)
+                nc.vector.quantize_mx(
+                    out=codes[:].bitcast(E4M3X4), scales=scales[:], in_=dealt[:, t0 * P * PACK : t1 * P * PACK]
+                )
+                for t in range(t0, t1):
+                    cols = slice((t - t0) * P, (t - t0 + 1) * P)
+                    operands[t] = (codes[:, cols], scales[:, cols])
+            return operands
 
         ul_dealt = sb.tile([P, FEATURES * PACK], BF16, name="ul_dealt", align_bytes=64)
-        ul_codes = sb.tile([P, FEATURES], U32, name="ul_codes", tag="ul_codes_then_planes", align_bytes=64)
-        ul_scales = sb.tile([P, FEATURES], U8, name="ul_scales", align_bytes=64)
         deal(nc.scalar.copy, ul_dealt, ul_raw[0], 0, 0, HALF)
         deal(nc.vector.tensor_copy, ul_dealt, ul_raw[1], 1, 0, HALF)
-        quantise_weights(ul_codes, ul_scales, ul_dealt, 2, 3)
-        quantise_weights(ul_codes, ul_scales, ul_dealt, 0, 2)
-        quantise_weights(ul_codes, ul_scales, ul_dealt, 3, 4)
+        ul_operands = quantise_weights(ul_dealt, "ul", "ul_codes_first")
 
-        def product(codes, scales, t, bank):
-            acc = ps.tile([P, PARENTS], F32, name="acc", tag="bank%d" % bank)
-            cols = slice(t * P, (t + 1) * P)
+        def product(operand, bank):
+            codes, scales = operand
+            acc = ps.tile([P, PARENTS], F32, name="acc", tag=bank)
             nc.tensor.matmul_mx(
                 out=acc[:],
-                lhsT=codes[:, cols].bitcast(E4M3X4),
-                lhsT_scale=scales[:, cols],
+                lhsT=codes.bitcast(E4M3X4),
+                lhsT_scale=scales,
                 rhs=dz_codes[:].bitcast(E5M2X4),
                 rhs_scale=dz_scales[:],
                 start=True,
@@ -108,52 +113,55 @@ def tile_attend_gtree_tnh_pl_kernel(tc, dh, h, ul, ur, loffs, roffs, out_0, out_
             )
             return acc
 
-        def scatter(acc, offsets, t, first, count, tag):
-            values = sb.tile([P, count], F32, name="values", tag=tag, align_bytes=64)
-            nc.scalar.copy(values[:], acc[:, first : first + count])
-            nc.vector.tensor_copy(windows[t][:].indirect(offsets[:, first // 16 : (first + count) // 16]), values[:])
+        def scatter(acc, offsets, t, first, values):
+            count = values.shape[1]
+            nc.scalar.copy(values, acc[:, first : first + count])
+            nc.vector.tensor_copy(windows[t][:].indirect(offsets[:, first // 16 : (first + count) // 16]), values)
 
-        first_acc = product(ul_codes, ul_scales, ORDER[0], 0)
-        scatter(first_acc, left_list, ORDER[0], 0, HALF, "values_first")
+        first_acc = product(ul_operands[ORDER[0]], "left0")
+        first_low = sb.tile([P, HALF], F32, name="first_low", align_bytes=64)
+        scatter(first_acc, left_list, ORDER[0], 0, first_low[:])
 
-        ur_dealt = sb.tile([P, FEATURES * PACK], BF16, name="ur_dealt", align_bytes=64)
-        ur_codes = sb.tile([P, FEATURES], U32, name="ur_codes", align_bytes=64)
-        ur_scales = sb.tile([P, FEATURES], U8, name="ur_scales", align_bytes=64)
-        for c in range(2):
-            for first in (0, HALF // 2):
-                deal(nc.scalar.copy, ur_dealt, ur_raw[c], c, first, HALF // 2)
-        quantise_weights(ur_codes, ur_scales, ur_dealt, 0, 4)
-        scatter(first_acc, left_list, ORDER[0], HALF, HALF, "ur_raw1")
+        ur_dealt = sb.tile([P, FEATURES * PACK], BF16, name="ur_dealt", tag="ul_dealt", align_bytes=64)
+        deal(nc.vector.tensor_copy, ur_dealt, ur_raw[0], 0, 0, HALF // 2)
+        deal(nc.scalar.copy, ur_dealt, ur_raw[0], 0, HALF // 2, HALF // 2)
+        deal(nc.scalar.copy, ur_dealt, ur_raw[1], 1, 0, HALF // 2)
+        deal(nc.scalar.copy, ur_dealt, ur_raw[1], 1, HALF // 2, HALF // 2)
+        ur_operands = quantise_weights(ur_dealt, "ur", "ur_codes_first")
+        first_high = sb.tile([P, HALF], F32, name="first_high", tag="ur_raw1", align_bytes=64)
+        scatter(first_acc, left_list, ORDER[0], HALF, first_high[:])
 
         out_rows = out_0.rearrange("(p t) n -> p t n", t=PACK)
-        chunks = [slice(k * CHUNK, (k + 1) * CHUNK) for k in range(NODES // CHUNK)]
+        chunks = [slice(0, 512), slice(512, 1024), slice(1024, 1536), slice(1536, 1792), slice(1792, 2048)]
+        grouped = sb.tile([P, NODES * PACK], BF16, name="grouped", align_bytes=64)
+        lanes = grouped[:].rearrange("p (n t) -> p n t", t=PACK)
 
         def left(step):
             t = ORDER[step]
-            scatter(product(ul_codes, ul_scales, t, step), left_list, t, 0, PARENTS, "values_left%d" % step)
+            values = left_values[:, (step - 1) * PARENTS : step * PARENTS]
+            scatter(product(ul_operands[t], "left%d" % step), left_list, t, 0, values)
 
-        def right(step, tag):
+        def right(step):
             t = ORDER[step]
-            scatter(product(ur_codes, ur_scales, t, step + 1), right_list, t, 0, PARENTS, tag)
+            values = sb.tile([P, PARENTS], F32, name="right_values%d" % step, align_bytes=64)
+            scatter(product(ur_operands[t], "right%d" % step), right_list, t, 0, values[:])
             nc.sync.dma_start(out=out_rows[:, t, :], in_=windows[t][:])
 
         def lane(step):
             t = ORDER[step]
-            for cols in chunks:
-                nc.scalar.copy(lanes[:, cols, t], windows[t][:, cols])
+            nc.scalar.copy(lanes[:, :, t], windows[t][:])
 
-        right(0, "values_right0")
+        right(0)
+        left_values = sb.tile([P, (PACK - 1) * PARENTS], F32, name="left_values", tag="ur_codes_first", align_bytes=64)
         for step in (1, 2):
             left(step)
-            right(step, "values_right%d" % step)
+            right(step)
         left(3)
-        grouped = sb.tile([P, NODES * PACK], BF16, name="grouped", tag="ul_codes_then_planes", align_bytes=64)
-        lanes = grouped[:].rearrange("p (n t) -> p n t", t=PACK)
         lane(0)
-        right(3, "values_right0")
+        right(3)
         lane(1)
         lane(2)
-        last = PACK - 1
+        last = ORDER[3]
         for k, cols in enumerate(chunks):
             copy = nc.vector.tensor_copy if k < 2 else nc.scalar.copy
             copy(lanes[:, cols, last], windows[last][:, cols])
@@ -161,11 +169,11 @@ def tile_attend_gtree_tnh_pl_kernel(tc, dh, h, ul, ur, loffs, roffs, out_0, out_
         out_words = out_1[0].rearrange("p n t -> p (n t)").bitcast(I32)
         out_scales = sb.tile([P, NODES], U8, name="out_scales", align_bytes=64)
         for k, cols in enumerate(chunks):
-            words = sb.tile([P, CHUNK], U32, name="words%d" % k, align_bytes=64)
+            words = sb.tile([P, cols.stop - cols.start], U32, name="words%d" % k, align_bytes=64)
             nc.vector.quantize_mx(
                 out=words[:].bitcast(E4M3X4),
                 scales=out_scales[:, cols],
-                in_=grouped[:, k * CHUNK * PACK : (k + 1) * CHUNK * PACK],
+                in_=grouped[:, cols.start * PACK : cols.stop * PACK],
             )
             nc.sync.dma_start(out=out_words[:, cols], in_=words[:].bitcast(I32))
         for q in range(4):

@@ -51,7 +51,11 @@ def tile_attend_gtree_tnh_pl_kernel(tc, dh, h, ul, ur, loffs, roffs, out_0, out_
 
         windows = [sb.tile([P, NODES], F32, name="window%d" % t, align_bytes=64) for t in range(PACK)]
         for t in ORDER:
-            nc.vector.memset(windows[t][:].bitcast(I32), 0)
+            if t in ORDER[:2]:
+                nc.vector.memset(windows[t][:, : NODES // 2 + 1], 0.0)
+                nc.vector.memset(windows[t][:, NODES // 2 + 1 :], 0.0)
+            else:
+                nc.gpsimd.memset(windows[t][:], 0.0)
 
         dz_codes = sb.tile([P, PARENTS], U32, name="dz_codes", align_bytes=64)
         dz_scales = sb.tile([P, PARENTS], U8, name="dz_scales", align_bytes=64)

@@ -42,8 +42,13 @@ def tile_attend_gtree_tnh_pl_kernel(tc, dh, h, ul, ur, loffs, roffs, out_0, out_
             nc.sync.dma_start(out=raw[:], in_=src.rearrange("(p j) w -> p j w", j=PACK)[:, :, c * HALF : (c + 1) * HALF])
             return raw
 
-        h_raw = [load_half(h, c, "h_raw%d" % c) for c in range(2)]
-        dh_raw = [load_half(dh, c, "dh_raw%d" % c) for c in range(2)]
+        h_raw = []
+        for c in range(2):
+            rows = sb.tile([P, 2, PARENTS], F32, name="h_raw%d" % c, align_bytes=64)
+            nc.sync.dma_start(out=rows[:], in_=h.rearrange("(p j) w -> p j w", j=PACK)[:, 2 * c : 2 * c + 2, :])
+            h_raw.append(rows)
+        dh_raw = sb.tile([P, PACK, PARENTS], F32, name="dh_raw", align_bytes=64)
+        nc.sync.dma_start(out=dh_raw[:], in_=dh.rearrange("(p j) w -> p j w", j=PACK))
         ul_raw = [load_half(ul, c, "ul_raw%d" % c) for c in range(2)]
         nc.sync.dma_start(left_list[:], loffs)
         ur_raw = [load_half(ur, c, "ur_raw%d" % c) for c in range(2)]
@@ -59,19 +64,17 @@ def tile_attend_gtree_tnh_pl_kernel(tc, dh, h, ul, ur, loffs, roffs, out_0, out_
 
         dz_codes = sb.tile([P, PARENTS], U32, name="dz_codes", align_bytes=64)
         dz_scales = sb.tile([P, PARENTS], U8, name="dz_scales", align_bytes=64)
+        slope = sb.tile([P, PACK, PARENTS], F32, name="slope", align_bytes=64)
         for c in range(2):
-            squares = sb.tile([P, PACK, HALF], F32, name="squares%d" % c, align_bytes=64)
+            squares = sb.tile([P, 2, PARENTS], F32, name="squares%d" % c, align_bytes=64)
             nc.scalar.activation(squares[:], h_raw[c][:], ACT.Square)
-            slope = sb.tile([P, PACK, HALF], F32, name="slope%d" % c, align_bytes=64)
-            if c == 0:
-                nc.vector.tensor_scalar(slope[:], squares[:], -1.0, 1.0, MULT, ADD)
-            else:
-                nc.scalar.activation(slope[:], squares[:], ACT.Copy, bias=1.0, scale=-1.0)
+            nc.vector.tensor_scalar(slope[:, 2 * c : 2 * c + 2, :], squares[:], -1.0, 1.0, MULT, ADD)
+        for c in range(2):
             dz = sb.tile([P, HALF * PACK], BF16, name="dz%d" % c, align_bytes=64)
             nc.vector.tensor_tensor(
                 dz[:].rearrange("p (c i j) -> p c j i", i=4, j=PACK),
-                dh_raw[c][:].rearrange("p j (c i) -> p c j i", i=4),
-                slope[:].rearrange("p j (c i) -> p c j i", i=4),
+                dh_raw[:, :, c * HALF : (c + 1) * HALF].rearrange("p j (c i) -> p c j i", i=4),
+                slope[:, :, c * HALF : (c + 1) * HALF].rearrange("p j (c i) -> p c j i", i=4),
                 MULT,
             )
             cols = slice(c * HALF, (c + 1) * HALF)

@@ -10,7 +10,7 @@ U16 = mybir.dt.uint16
 U8 = mybir.dt.uint8
 E4M3X4 = mybir.dt.float8_e4m3fn_x4
 E5M2X4 = mybir.dt.float8_e5m2_x4
-ACT = mybir.ActivationFunctionType
+SQUARE = mybir.ActivationFunctionType.Square
 MULT = mybir.AluOpType.mult
 ADD = mybir.AluOpType.add
 
@@ -20,12 +20,19 @@ PARENTS = 512
 FEATURES = 512
 NODES = 2048
 HALF = 256
-CHUNK = 512
-LIST_COLS = PARENTS // 16
+QUARTER = 128
+LINE = 4
+BAND = 16
+QUADRANT = 32
+ALIGN = 64
 
 ORDER = (1, 2, 3, 0)
+LANE_RUNS = ((1, 2), (2, 4), (0, 1))
+UL_SCALAR_COLUMNS = 96
+TAIL_CHUNKS = (slice(0, 512), slice(512, 1024), slice(1024, 1536), slice(1536, 1792), slice(1792, 2048))
+VECTOR_TAIL_CHUNKS = 2
 
-FLOPS = 2 * 2 * 512 * 512 * 512
+FLOPS = 2 * 2 * 512 * FEATURES * PARENTS
 
 
 def tile_attend_gtree_tnh_pl_kernel(tc, dh, h, ul, ur, loffs, roffs, out_0, out_1, out_2):
@@ -34,51 +41,56 @@ def tile_attend_gtree_tnh_pl_kernel(tc, dh, h, ul, ur, loffs, roffs, out_0, out_
         sb = ctx.enter_context(tc.tile_pool(name="sb", bufs=1))
         ps = ctx.enter_context(tc.psum_pool(name="ps", bufs=1))
 
-        left_list = sb.tile([P, LIST_COLS], U16, name="left_list")
-        right_list = sb.tile([P, LIST_COLS], U16, name="right_list")
+        left_list = sb.tile([P, PARENTS // BAND], U16, name="left_list")
+        right_list = sb.tile([P, PARENTS // BAND], U16, name="right_list")
 
-        def load_half(src, c, name):
-            raw = sb.tile([P, PACK, HALF], F32, name=name, align_bytes=64)
-            nc.sync.dma_start(out=raw[:], in_=src.rearrange("(p j) w -> p j w", j=PACK)[:, :, c * HALF : (c + 1) * HALF])
+        def rows_of(matrix):
+            return matrix.rearrange("(p j) w -> p j w", j=PACK)
+
+        def load_half(matrix, c, name):
+            raw = sb.tile([P, PACK, HALF], F32, name=name, align_bytes=ALIGN)
+            nc.sync.dma_start(out=raw[:], in_=rows_of(matrix)[:, :, c * HALF : (c + 1) * HALF])
             return raw
 
+        row_pairs = [slice(0, PACK // 2), slice(PACK // 2, PACK)]
         h_raw = []
-        for c in range(2):
-            rows = sb.tile([P, 2, PARENTS], F32, name="h_raw%d" % c, align_bytes=64)
-            nc.sync.dma_start(out=rows[:], in_=h.rearrange("(p j) w -> p j w", j=PACK)[:, 2 * c : 2 * c + 2, :])
+        for c, pair in enumerate(row_pairs):
+            rows = sb.tile([P, PACK // 2, PARENTS], F32, name="h_raw%d" % c, align_bytes=ALIGN)
+            nc.sync.dma_start(out=rows[:], in_=rows_of(h)[:, pair, :])
             h_raw.append(rows)
-        dh_raw = sb.tile([P, PACK, PARENTS], F32, name="dh_raw", align_bytes=64)
-        nc.sync.dma_start(out=dh_raw[:], in_=dh.rearrange("(p j) w -> p j w", j=PACK))
+        dh_raw = sb.tile([P, PACK, PARENTS], F32, name="dh_raw", align_bytes=ALIGN)
+        nc.sync.dma_start(out=dh_raw[:], in_=rows_of(dh))
         ul_raw = [load_half(ul, c, "ul_raw%d" % c) for c in range(2)]
         nc.sync.dma_start(left_list[:], loffs)
         ur_raw = [load_half(ur, c, "ur_raw%d" % c) for c in range(2)]
         nc.sync.dma_start(right_list[:], roffs)
 
-        windows = [sb.tile([P, NODES], F32, name="window%d" % t, align_bytes=64) for t in range(PACK)]
+        windows = [sb.tile([P, NODES], F32, name="window%d" % t, align_bytes=ALIGN) for t in range(PACK)]
+        odd_cut = NODES // 2 + 1
         for t in ORDER:
-            if t in ORDER[:2]:
-                nc.vector.memset(windows[t][:, : NODES // 2 + 1], 0.0)
-                nc.vector.memset(windows[t][:, NODES // 2 + 1 :], 0.0)
+            if t in ORDER[: PACK // 2]:
+                nc.vector.memset(windows[t][:, :odd_cut], 0.0)
+                nc.vector.memset(windows[t][:, odd_cut:], 0.0)
             else:
                 nc.gpsimd.memset(windows[t][:], 0.0)
 
-        dz_codes = sb.tile([P, PARENTS], U32, name="dz_codes", align_bytes=64)
-        dz_scales = sb.tile([P, PARENTS], U8, name="dz_scales", align_bytes=64)
-        slope = sb.tile([P, PACK, PARENTS], F32, name="slope", align_bytes=64)
+        dz_codes = sb.tile([P, PARENTS], U32, name="dz_codes", align_bytes=ALIGN)
+        dz_scales = sb.tile([P, PARENTS], U8, name="dz_scales", align_bytes=ALIGN)
+        slope = sb.tile([P, PACK, PARENTS], F32, name="slope", align_bytes=ALIGN)
+        for c, pair in enumerate(row_pairs):
+            squares = sb.tile([P, PACK // 2, PARENTS], F32, name="squares%d" % c, align_bytes=ALIGN)
+            nc.scalar.activation(squares[:], h_raw[c][:], SQUARE)
+            nc.vector.tensor_scalar(slope[:, pair, :], squares[:], -1.0, 1.0, MULT, ADD)
         for c in range(2):
-            squares = sb.tile([P, 2, PARENTS], F32, name="squares%d" % c, align_bytes=64)
-            nc.scalar.activation(squares[:], h_raw[c][:], ACT.Square)
-            nc.vector.tensor_scalar(slope[:, 2 * c : 2 * c + 2, :], squares[:], -1.0, 1.0, MULT, ADD)
-        for c in range(2):
-            dz = sb.tile([P, HALF * PACK], BF16, name="dz%d" % c, align_bytes=64)
+            parents = slice(c * HALF, (c + 1) * HALF)
+            dz = sb.tile([P, HALF * PACK], BF16, name="dz%d" % c, align_bytes=ALIGN)
             nc.vector.tensor_tensor(
-                dz[:].rearrange("p (c i j) -> p c j i", i=4, j=PACK),
-                dh_raw[:, :, c * HALF : (c + 1) * HALF].rearrange("p j (c i) -> p c j i", i=4),
-                slope[:, :, c * HALF : (c + 1) * HALF].rearrange("p j (c i) -> p c j i", i=4),
+                dz[:].rearrange("p (c i j) -> p c j i", i=LINE, j=PACK),
+                dh_raw[:, :, parents].rearrange("p j (c i) -> p c j i", i=LINE),
+                slope[:, :, parents].rearrange("p j (c i) -> p c j i", i=LINE),
                 MULT,
             )
-            cols = slice(c * HALF, (c + 1) * HALF)
-            nc.vector.quantize_mx(out=dz_codes[:, cols].bitcast(E5M2X4), scales=dz_scales[:, cols], in_=dz[:])
+            nc.vector.quantize_mx(out=dz_codes[:, parents].bitcast(E5M2X4), scales=dz_scales[:, parents], in_=dz[:])
 
         def deal(copy, dealt, raw, c, first, count):
             m0 = (c * HALF + first) // PACK
@@ -87,12 +99,11 @@ def tile_attend_gtree_tnh_pl_kernel(tc, dh, h, ul, ur, loffs, roffs, out_0, out_
                 raw[:, :, first : first + count].rearrange("p j (m t) -> p m t j", t=PACK),
             )
 
-        def quantise_weights(dealt, name, first_tag):
+        def quantise_weights(dealt, name):
             operands = {}
-            for t0, t1 in ((1, 2), (2, 4), (0, 1)):
-                tag = first_tag if t0 == ORDER[0] else "%s_codes%d" % (name, t0)
-                codes = sb.tile([P, (t1 - t0) * P], U32, name="codes", tag=tag, align_bytes=64)
-                scales = sb.tile([P, (t1 - t0) * P], U8, name="scales", tag="%s_scales%d" % (name, t0), align_bytes=64)
+            for t0, t1 in LANE_RUNS:
+                codes = sb.tile([P, (t1 - t0) * P], U32, name="%s_codes%d" % (name, t0), align_bytes=ALIGN)
+                scales = sb.tile([P, (t1 - t0) * P], U8, name="%s_scales%d" % (name, t0), align_bytes=ALIGN)
                 nc.vector.quantize_mx(
                     out=codes[:].bitcast(E4M3X4), scales=scales[:], in_=dealt[:, t0 * P * PACK : t1 * P * PACK]
                 )
@@ -100,11 +111,6 @@ def tile_attend_gtree_tnh_pl_kernel(tc, dh, h, ul, ur, loffs, roffs, out_0, out_
                     cols = slice((t - t0) * P, (t - t0 + 1) * P)
                     operands[t] = (codes[:, cols], scales[:, cols])
             return operands
-
-        ul_dealt = sb.tile([P, FEATURES * PACK], BF16, name="ul_dealt", align_bytes=64)
-        deal(nc.scalar.copy, ul_dealt, ul_raw[0], 0, 0, HALF)
-        deal(nc.vector.tensor_copy, ul_dealt, ul_raw[1], 1, 0, HALF)
-        ul_operands = quantise_weights(ul_dealt, "ul", "ul_codes_first")
 
         def product(operand, bank):
             codes, scales = operand
@@ -123,68 +129,77 @@ def tile_attend_gtree_tnh_pl_kernel(tc, dh, h, ul, ur, loffs, roffs, out_0, out_
         def scatter(acc, offsets, t, first, values):
             count = values.shape[1]
             nc.scalar.copy(values, acc[:, first : first + count])
-            nc.vector.tensor_copy(windows[t][:].indirect(offsets[:, first // 16 : (first + count) // 16]), values)
+            entries = offsets[:, first // BAND : (first + count) // BAND]
+            nc.vector.tensor_copy(windows[t][:].indirect(entries), values)
+
+        ul_dealt = sb.tile([P, FEATURES * PACK], BF16, name="ul_dealt", align_bytes=ALIGN)
+        deal(nc.scalar.copy, ul_dealt, ul_raw[0], 0, 0, HALF)
+        deal(nc.scalar.copy, ul_dealt, ul_raw[1], 1, 0, UL_SCALAR_COLUMNS)
+        deal(nc.vector.tensor_copy, ul_dealt, ul_raw[1], 1, UL_SCALAR_COLUMNS, HALF - UL_SCALAR_COLUMNS)
+        ul_operands = quantise_weights(ul_dealt, "ul")
 
         first_acc = product(ul_operands[ORDER[0]], "left0")
-        first_low = sb.tile([P, HALF], F32, name="first_low", align_bytes=64)
+        first_low = sb.tile([P, HALF], F32, name="first_low", align_bytes=ALIGN)
         scatter(first_acc, left_list, ORDER[0], 0, first_low[:])
 
-        ur_dealt = sb.tile([P, FEATURES * PACK], BF16, name="ur_dealt", tag="ul_dealt", align_bytes=64)
-        deal(nc.vector.tensor_copy, ur_dealt, ur_raw[0], 0, 0, HALF // 2)
-        deal(nc.scalar.copy, ur_dealt, ur_raw[0], 0, HALF // 2, HALF // 2)
-        deal(nc.scalar.copy, ur_dealt, ur_raw[1], 1, 0, HALF // 2)
-        deal(nc.scalar.copy, ur_dealt, ur_raw[1], 1, HALF // 2, HALF // 2)
-        ur_operands = quantise_weights(ur_dealt, "ur", "ur_codes_first")
-        first_high = sb.tile([P, HALF], F32, name="first_high", tag="ur_raw1", align_bytes=64)
+        ur_dealt = sb.tile([P, FEATURES * PACK], BF16, name="ur_dealt", tag="ul_dealt", align_bytes=ALIGN)
+        deal(nc.vector.tensor_copy, ur_dealt, ur_raw[0], 0, 0, QUARTER)
+        deal(nc.scalar.copy, ur_dealt, ur_raw[0], 0, QUARTER, QUARTER)
+        deal(nc.scalar.copy, ur_dealt, ur_raw[1], 1, 0, QUARTER)
+        deal(nc.scalar.copy, ur_dealt, ur_raw[1], 1, QUARTER, QUARTER)
+        ur_operands = quantise_weights(ur_dealt, "ur")
+        first_high = sb.tile([P, HALF], F32, name="first_high", tag="ur_raw1", align_bytes=ALIGN)
         scatter(first_acc, left_list, ORDER[0], HALF, first_high[:])
 
         out_rows = out_0.rearrange("(p t) n -> p t n", t=PACK)
-        chunks = [slice(0, 512), slice(512, 1024), slice(1024, 1536), slice(1536, 1792), slice(1792, 2048)]
-        grouped = sb.tile([P, NODES * PACK], BF16, name="grouped", align_bytes=64)
+        grouped = sb.tile([P, NODES * PACK], BF16, name="grouped", align_bytes=ALIGN)
         lanes = grouped[:].rearrange("p (n t) -> p n t", t=PACK)
 
-        def left(step):
+        def scatter_left(step):
             t = ORDER[step]
             values = left_values[:, (step - 1) * PARENTS : step * PARENTS]
             scatter(product(ul_operands[t], "left%d" % step), left_list, t, 0, values)
 
-        def right(step):
+        def scatter_right_and_store(step):
             t = ORDER[step]
-            values = sb.tile([P, PARENTS], F32, name="right_values%d" % step, align_bytes=64)
+            values = sb.tile([P, PARENTS], F32, name="right_values%d" % step, align_bytes=ALIGN)
             scatter(product(ur_operands[t], "right%d" % step), right_list, t, 0, values[:])
             nc.sync.dma_start(out=out_rows[:, t, :], in_=windows[t][:])
 
-        def lane(step):
+        def write_lane(step):
             t = ORDER[step]
             nc.scalar.copy(lanes[:, :, t], windows[t][:])
 
-        right(0)
-        left_values = sb.tile([P, (PACK - 1) * PARENTS], F32, name="left_values", tag="ur_codes_first", align_bytes=64)
-        for step in (1, 2):
-            left(step)
-            right(step)
-        left(3)
-        lane(0)
-        right(3)
-        lane(1)
-        lane(2)
-        last = ORDER[3]
-        for k, cols in enumerate(chunks):
-            copy = nc.vector.tensor_copy if k < 2 else nc.scalar.copy
-            copy(lanes[:, cols, last], windows[last][:, cols])
+        scatter_right_and_store(0)
+        left_values = sb.tile(
+            [P, (PACK - 1) * PARENTS], F32, name="left_values", tag="ur_codes%d" % ORDER[0], align_bytes=ALIGN
+        )
+        last = PACK - 1
+        for step in range(1, last):
+            scatter_left(step)
+            scatter_right_and_store(step)
+        scatter_left(last)
+        write_lane(0)
+        scatter_right_and_store(last)
+        for step in range(1, last):
+            write_lane(step)
+        for k, cols in enumerate(TAIL_CHUNKS):
+            copy = nc.vector.tensor_copy if k < VECTOR_TAIL_CHUNKS else nc.scalar.copy
+            copy(lanes[:, cols, ORDER[last]], windows[ORDER[last]][:, cols])
 
         out_words = out_1[0].rearrange("p n t -> p (n t)").bitcast(I32)
-        out_scales = sb.tile([P, NODES], U8, name="out_scales", align_bytes=64)
-        for k, cols in enumerate(chunks):
-            words = sb.tile([P, cols.stop - cols.start], U32, name="words%d" % k, align_bytes=64)
+        out_scales = sb.tile([P, NODES], U8, name="out_scales", align_bytes=ALIGN)
+        for k, cols in enumerate(TAIL_CHUNKS):
+            words = sb.tile([P, cols.stop - cols.start], U32, name="words%d" % k, align_bytes=ALIGN)
             nc.vector.quantize_mx(
                 out=words[:].bitcast(E4M3X4),
                 scales=out_scales[:, cols],
                 in_=grouped[:, cols.start * PACK : cols.stop * PACK],
             )
             nc.sync.dma_start(out=out_words[:, cols], in_=words[:].bitcast(I32))
-        for q in range(4):
+        scale_rows = QUADRANT // 8
+        for q in range(P // QUADRANT):
             nc.scalar.dma_start(
-                out=out_2[0, 4 * q : 4 * q + 4, :].bitcast(I32),
-                in_=out_scales[32 * q : 32 * q + 4, :].bitcast(I32),
+                out=out_2[0, scale_rows * q : scale_rows * (q + 1), :].bitcast(I32),
+                in_=out_scales[QUADRANT * q : QUADRANT * q + scale_rows, :].bitcast(I32),
             )

from contextlib import ExitStack

import concourse.mybir as mybir

F32 = mybir.dt.float32
BF16 = mybir.dt.bfloat16
I32 = mybir.dt.int32
U32 = mybir.dt.uint32
U16 = mybir.dt.uint16
U8 = mybir.dt.uint8
E4M3X4 = mybir.dt.float8_e4m3fn_x4
E5M2X4 = mybir.dt.float8_e5m2_x4
SQUARE = mybir.ActivationFunctionType.Square
MULT = mybir.AluOpType.mult
ADD = mybir.AluOpType.add

P = 128
PACK = 4
PARENTS = 512
FEATURES = 512
NODES = 2048
HALF = 256
QUARTER = 128
LINE = 4
BAND = 16
QUADRANT = 32
ALIGN = 64

ORDER = (1, 2, 3, 0)
LANE_RUNS = ((1, 2), (2, 4), (0, 1))
UL_SCALAR_COLUMNS = 96
TAIL_CHUNKS = (slice(0, 512), slice(512, 1024), slice(1024, 1536), slice(1536, 1792), slice(1792, 2048))
VECTOR_TAIL_CHUNKS = 2

FLOPS = 2 * 2 * 512 * FEATURES * PARENTS


def tile_attend_gtree_tnh_pl_kernel(tc, dh, h, ul, ur, loffs, roffs, out_0, out_1, out_2):
    nc = tc.nc
    with ExitStack() as ctx:
        sb = ctx.enter_context(tc.tile_pool(name="sb", bufs=1))
        ps = ctx.enter_context(tc.psum_pool(name="ps", bufs=1))

        left_list = sb.tile([P, PARENTS // BAND], U16, name="left_list")
        right_list = sb.tile([P, PARENTS // BAND], U16, name="right_list")

        def rows_of(matrix):
            return matrix.rearrange("(p j) w -> p j w", j=PACK)

        def load_half(matrix, c, name):
            raw = sb.tile([P, PACK, HALF], F32, name=name, align_bytes=ALIGN)
            nc.sync.dma_start(out=raw[:], in_=rows_of(matrix)[:, :, c * HALF : (c + 1) * HALF])
            return raw

        row_pairs = [slice(0, PACK // 2), slice(PACK // 2, PACK)]
        h_raw = []
        for c, pair in enumerate(row_pairs):
            rows = sb.tile([P, PACK // 2, PARENTS], F32, name="h_raw%d" % c, align_bytes=ALIGN)
            nc.sync.dma_start(out=rows[:], in_=rows_of(h)[:, pair, :])
            h_raw.append(rows)
        dh_raw = sb.tile([P, PACK, PARENTS], F32, name="dh_raw", align_bytes=ALIGN)
        nc.sync.dma_start(out=dh_raw[:], in_=rows_of(dh))
        ul_raw = [load_half(ul, c, "ul_raw%d" % c) for c in range(2)]
        nc.sync.dma_start(left_list[:], loffs)
        ur_raw = [load_half(ur, c, "ur_raw%d" % c) for c in range(2)]
        nc.sync.dma_start(right_list[:], roffs)

        windows = [sb.tile([P, NODES], F32, name="window%d" % t, align_bytes=ALIGN) for t in range(PACK)]
        odd_cut = NODES // 2 + 1
        for t in ORDER:
            if t in ORDER[: PACK // 2]:
                nc.vector.memset(windows[t][:, :odd_cut], 0.0)
                nc.vector.memset(windows[t][:, odd_cut:], 0.0)
            else:
                nc.gpsimd.memset(windows[t][:], 0.0)

        dz_codes = sb.tile([P, PARENTS], U32, name="dz_codes", align_bytes=ALIGN)
        dz_scales = sb.tile([P, PARENTS], U8, name="dz_scales", align_bytes=ALIGN)
        slope = sb.tile([P, PACK, PARENTS], F32, name="slope", align_bytes=ALIGN)
        for c, pair in enumerate(row_pairs):
            squares = sb.tile([P, PACK // 2, PARENTS], F32, name="squares%d" % c, align_bytes=ALIGN)
            nc.scalar.activation(squares[:], h_raw[c][:], SQUARE)
            nc.vector.tensor_scalar(slope[:, pair, :], squares[:], -1.0, 1.0, MULT, ADD)
        for c in range(2):
            parents = slice(c * HALF, (c + 1) * HALF)
            dz = sb.tile([P, HALF * PACK], BF16, name="dz%d" % c, align_bytes=ALIGN)
            nc.vector.tensor_tensor(
                dz[:].rearrange("p (c i j) -> p c j i", i=LINE, j=PACK),
                dh_raw[:, :, parents].rearrange("p j (c i) -> p c j i", i=LINE),
                slope[:, :, parents].rearrange("p j (c i) -> p c j i", i=LINE),
                MULT,
            )
            nc.vector.quantize_mx(out=dz_codes[:, parents].bitcast(E5M2X4), scales=dz_scales[:, parents], in_=dz[:])

        def deal(copy, dealt, raw, c, first, count):
            m0 = (c * HALF + first) // PACK
            copy(
                dealt[:].rearrange("p (t m j) -> p m t j", t=PACK, j=PACK)[:, m0 : m0 + count // PACK],
                raw[:, :, first : first + count].rearrange("p j (m t) -> p m t j", t=PACK),
            )

        def quantise_weights(dealt, name):
            operands = {}
            for t0, t1 in LANE_RUNS:
                codes = sb.tile([P, (t1 - t0) * P], U32, name="%s_codes%d" % (name, t0), align_bytes=ALIGN)
                scales = sb.tile([P, (t1 - t0) * P], U8, name="%s_scales%d" % (name, t0), align_bytes=ALIGN)
                nc.vector.quantize_mx(
                    out=codes[:].bitcast(E4M3X4), scales=scales[:], in_=dealt[:, t0 * P * PACK : t1 * P * PACK]
                )
                for t in range(t0, t1):
                    cols = slice((t - t0) * P, (t - t0 + 1) * P)
                    operands[t] = (codes[:, cols], scales[:, cols])
            return operands

        def product(operand, bank):
            codes, scales = operand
            acc = ps.tile([P, PARENTS], F32, name="acc", tag=bank)
            nc.tensor.matmul_mx(
                out=acc[:],
                lhsT=codes.bitcast(E4M3X4),
                lhsT_scale=scales,
                rhs=dz_codes[:].bitcast(E5M2X4),
                rhs_scale=dz_scales[:],
                start=True,
                stop=True,
            )
            return acc

        def scatter(acc, offsets, t, first, values):
            count = values.shape[1]
            nc.scalar.copy(values, acc[:, first : first + count])
            entries = offsets[:, first // BAND : (first + count) // BAND]
            nc.vector.tensor_copy(windows[t][:].indirect(entries), values)

        ul_dealt = sb.tile([P, FEATURES * PACK], BF16, name="ul_dealt", align_bytes=ALIGN)
        deal(nc.scalar.copy, ul_dealt, ul_raw[0], 0, 0, HALF)
        deal(nc.scalar.copy, ul_dealt, ul_raw[1], 1, 0, UL_SCALAR_COLUMNS)
        deal(nc.vector.tensor_copy, ul_dealt, ul_raw[1], 1, UL_SCALAR_COLUMNS, HALF - UL_SCALAR_COLUMNS)
        ul_operands = quantise_weights(ul_dealt, "ul")

        first_acc = product(ul_operands[ORDER[0]], "left0")
        first_low = sb.tile([P, HALF], F32, name="first_low", align_bytes=ALIGN)
        scatter(first_acc, left_list, ORDER[0], 0, first_low[:])

        ur_dealt = sb.tile([P, FEATURES * PACK], BF16, name="ur_dealt", tag="ul_dealt", align_bytes=ALIGN)
        deal(nc.vector.tensor_copy, ur_dealt, ur_raw[0], 0, 0, QUARTER)
        deal(nc.scalar.copy, ur_dealt, ur_raw[0], 0, QUARTER, QUARTER)
        deal(nc.scalar.copy, ur_dealt, ur_raw[1], 1, 0, QUARTER)
        deal(nc.scalar.copy, ur_dealt, ur_raw[1], 1, QUARTER, QUARTER)
        ur_operands = quantise_weights(ur_dealt, "ur")
        first_high = sb.tile([P, HALF], F32, name="first_high", tag="ur_raw1", align_bytes=ALIGN)
        scatter(first_acc, left_list, ORDER[0], HALF, first_high[:])

        out_rows = out_0.rearrange("(p t) n -> p t n", t=PACK)
        grouped = sb.tile([P, NODES * PACK], BF16, name="grouped", align_bytes=ALIGN)
        lanes = grouped[:].rearrange("p (n t) -> p n t", t=PACK)

        def scatter_left(step):
            t = ORDER[step]
            values = left_values[:, (step - 1) * PARENTS : step * PARENTS]
            scatter(product(ul_operands[t], "left%d" % step), left_list, t, 0, values)

        def scatter_right_and_store(step):
            t = ORDER[step]
            values = sb.tile([P, PARENTS], F32, name="right_values%d" % step, align_bytes=ALIGN)
            scatter(product(ur_operands[t], "right%d" % step), right_list, t, 0, values[:])
            nc.sync.dma_start(out=out_rows[:, t, :], in_=windows[t][:])

        def write_lane(step):
            t = ORDER[step]
            nc.scalar.copy(lanes[:, :, t], windows[t][:])

        scatter_right_and_store(0)
        left_values = sb.tile(
            [P, (PACK - 1) * PARENTS], F32, name="left_values", tag="ur_codes%d" % ORDER[0], align_bytes=ALIGN
        )
        last = PACK - 1
        for step in range(1, last):
            scatter_left(step)
            scatter_right_and_store(step)
        scatter_left(last)
        write_lane(0)
        scatter_right_and_store(last)
        for step in range(1, last):
            write_lane(step)
        for k, cols in enumerate(TAIL_CHUNKS):
            copy = nc.vector.tensor_copy if k < VECTOR_TAIL_CHUNKS else nc.scalar.copy
            copy(lanes[:, cols, ORDER[last]], windows[ORDER[last]][:, cols])

        out_words = out_1[0].rearrange("p n t -> p (n t)").bitcast(I32)
        out_scales = sb.tile([P, NODES], U8, name="out_scales", align_bytes=ALIGN)
        for k, cols in enumerate(TAIL_CHUNKS):
            words = sb.tile([P, cols.stop - cols.start], U32, name="words%d" % k, align_bytes=ALIGN)
            nc.vector.quantize_mx(
                out=words[:].bitcast(E4M3X4),
                scales=out_scales[:, cols],
                in_=grouped[:, cols.start * PACK : cols.stop * PACK],
            )
            nc.sync.dma_start(out=out_words[:, cols], in_=words[:].bitcast(I32))
        scale_rows = QUADRANT // 8
        for q in range(P // QUADRANT):
            nc.scalar.dma_start(
                out=out_2[0, scale_rows * q : scale_rows * (q + 1), :].bitcast(I32),
                in_=out_scales[QUADRANT * q : QUADRANT * q + scale_rows, :].bitcast(I32),
            )
